import numpy as np
import ml_dtypes


def mxq(x, axis, fmt="e4m3"):
    dtype, down = {"e4m3": (ml_dtypes.float8_e4m3fn, 7), "e5m2": (ml_dtypes.float8_e5m2, 14)}[fmt]
    v = np.moveaxis(np.asarray(x, np.float32).astype(ml_dtypes.bfloat16).astype(np.float64), axis, -1)
    blocks = v.reshape(v.shape[:-1] + (-1, 32))
    amax = np.abs(blocks).max(-1, keepdims=True)
    byte = np.maximum(np.where(amax > 0, np.frexp(amax)[1] - 1 + 127, 0) - down, 1)
    scale = np.exp2(byte - 127.0)
    codes = (blocks / scale).astype(np.float32).astype(dtype).astype(np.float64)
    return np.moveaxis((codes * scale).reshape(v.shape), -1, axis)


WIDE = False


def mx_kscale(k):
    if not WIDE:
        return np.ones(k)
    levels = np.array([30, -30])
    if k % 512:
        return np.exp2(np.random.permutation(np.resize(levels, k // 32))).repeat(32)
    a = np.empty((k // 512, 16))
    for p in range(k // 512):
        a[p, :8] = np.random.permutation(np.resize(levels, 8))
        for g in range(8):
            far = levels[np.abs(levels - a[p, g]) >= 10]
            a[p, g + 8] = far[np.random.randint(len(far))]
    return np.exp2(a.ravel()).repeat(32)


def f64(x):
    return np.asarray(x).astype(np.float64)


def striped(idx):
    return np.tile(np.asarray(idx).reshape(-1, 16).T, (8, 1)).astype(np.uint16)


def unstriped(offs):
    return offs[:16].T.reshape(-1).astype(np.int64)


E2M1 = np.array([0.0, 0.5, 1.0, 1.5, 2.0, 3.0, 4.0, 6.0, -0.0, -0.5, -1.0, -1.5, -2.0, -3.0, -4.0, -6.0])


def pack_weight(w, fmt):
    k, n = w.shape
    w = f64(np.asarray(w, np.float32).astype(ml_dtypes.bfloat16)).reshape(k // 32, 32, n)
    amax = np.abs(w).max(1)
    if fmt in ("e4m3", "e5m2"):
        byte = np.frexp(amax)[1] - 1 + 127 - (7 if fmt == "e4m3" else 14)
    else:
        mant, ex = np.frexp(amax / 6.0)
        byte = np.where(mant > 0.5, ex, ex - 1) + 127
    byte = np.clip(np.where(amax > 0, byte, 1), 1, 254)
    scaled = (w * np.exp2(127.0 - byte)[:, None, :]).reshape(k, n).astype(np.float32)
    by_word = np.ascontiguousarray(scaled.reshape(k // 512, 128, 4, n).transpose(0, 1, 3, 2))
    if fmt in ("e4m3", "e5m2"):
        words = by_word.astype(ml_dtypes.float8_e4m3fn if fmt == "e4m3" else ml_dtypes.float8_e5m2).view(np.uint8)
    else:
        c = by_word.astype(ml_dtypes.float4_e2m1fn).view(np.uint8) & 0xF
        words = (c[..., 0::2] | (c[..., 1::2] << 4)).reshape(k // 512, 128, 2 * n)
    return np.ascontiguousarray(words), np.ascontiguousarray(byte.astype(np.uint8).reshape(k // 512, 16, n))


def unpack_weight(words, scales, fmt):
    g, _, n = scales.shape
    words = np.ascontiguousarray(words).reshape(g, 128, n, -1)
    if fmt in ("e4m3", "e5m2"):
        vals = words.view(ml_dtypes.float8_e4m3fn if fmt == "e4m3" else ml_dtypes.float8_e5m2).astype(np.float64)
    else:
        nib = np.empty((g, 128, n, 4), np.uint8)
        nib[..., 0::2] = words & 0xF
        nib[..., 1::2] = words >> 4
        vals = E2M1[nib]
    vals = vals * np.repeat(np.exp2(scales.astype(np.float64) - 127.0), 8, axis=1)[..., None]
    return vals.transpose(0, 1, 3, 2).reshape(g * 512, n)


K, T, J, N, L = 1024, 1024, 256, 256, 512


def setup_inputs():
    n = np.random.standard_normal
    idx = np.random.permutation(T)[:J]
    fk = mx_kscale(K)
    fl = mx_kscale(L)
    xtp = pack_weight(n((K, T)) * np.random.uniform(0.4, 1.6, (1, T)) / fk[:, None], "e2m1")
    wap = pack_weight(n((K, N)) * 1 / np.sqrt(K) * fk[:, None], "e5m2")
    wbp = pack_weight(n((L, N)) * 1 / np.sqrt(L) * fl[:, None], "e4m3")
    return {
        "xt_words": xtp[0],
        "xt_scales": xtp[1],
        "wa_words": wap[0],
        "wa_scales": wap[1],
        "sx": (n((L, J)) * np.random.uniform(0.4, 1.6, (1, J)) / fl[:, None]).astype(np.float32),
        "wb_words": wbp[0],
        "wb_scales": wbp[1],
        "bi": (np.random.uniform(-0.6, 0.6, (1, N))).astype(np.float32),
        "gm": (np.random.uniform(0.5, 2.0, (1, N))).astype(np.float32),
        "offs": striped(idx),
    }


def reference(xt_words, xt_scales, wa_words, wa_scales, sx, wb_words, wb_scales, bi, gm, offs):
    idx = unstriped(offs)
    xtu = unpack_weight(xt_words, xt_scales, "e2m1")
    wau = unpack_weight(wa_words, wa_scales, "e5m2")
    wbu = unpack_weight(wb_words, wb_scales, "e4m3")
    xtidxg = xtu[:, idx]
    a = xtidxg.T @ wau
    sxq = mxq(f64(sx), 0, "e5m2")
    b0 = sxq.T @ wbu
    b2 = b0 + f64(bi)
    d1 = np.mean(np.square(a - b2), axis=1, keepdims=True)
    y = a * f64(gm) / (0.4 + d1)
    return y

@@ -1,0 +1,146 @@
+import math
+from contextlib import ExitStack
+
+import concourse.mybir as mybir
+from concourse.masks import make_identity
+
+K, T, J, N, L = 1024, 1024, 256, 256, 512
+FLOPS = 2 * J * K * N + 2 * J * L * N
+
+F32 = mybir.dt.float32
+BF16 = mybir.dt.bfloat16
+I32 = mybir.dt.int32
+U32 = mybir.dt.uint32
+U16 = mybir.dt.uint16
+U8 = mybir.dt.uint8
+E2M1 = mybir.dt.float4_e2m1fn_x4
+E5M2 = mybir.dt.float8_e5m2_x4
+E4M3 = mybir.dt.float8_e4m3fn_x4
+ALU = mybir.AluOpType
+ACT = mybir.ActivationFunctionType
+
+P = 128
+PASSES = K // 512
+TILES = J // P
+OFFSET = 0.4
+
+
+def tile_list_rows_owninput_bygapsize_kernel(
+    tc, xt_words, xt_scales, wa_words, wa_scales, sx, wb_words, wb_scales, bi, gm, offs, out
+):
+    nc = tc.nc
+    with ExitStack() as ctx:
+        sb = ctx.enter_context(tc.tile_pool(name="sb", bufs=1))
+        ps = ctx.enter_context(tc.psum_pool(name="ps", bufs=1))
+
+        offsets = sb.tile([P, J // 16], U16, name="offsets")
+        xw = [sb.tile([P, T], U16, name="xw%d" % z, align_bytes=64) for z in range(PASSES)]
+        xs = sb.tile([P, PASSES * T], U8, name="xs", align_bytes=64)
+        gw = [sb.tile([P, J], U16, name="gw%d" % z, align_bytes=64) for z in range(PASSES)]
+        gs = [sb.tile([P, J], U8, name="gs%d" % z, align_bytes=64) for z in range(PASSES)]
+        waw = sb.tile([P, PASSES * N], U32, name="waw", align_bytes=64)
+        was = sb.tile([P, PASSES * N], U8, name="was", align_bytes=64)
+        wbw = sb.tile([P, N], U32, name="wbw", align_bytes=64)
+        wbs = sb.tile([P, N], U8, name="wbs", align_bytes=64)
+        raw = sb.tile([P, 4, J], F32, name="raw", tag="raw")
+        grouped = sb.tile([P, J, 4], BF16, name="grouped", align_bytes=64)
+        sxw = sb.tile([P, J], U32, name="sxw", align_bytes=64)
+        sxs = sb.tile([P, J], U8, name="sxs", align_bytes=64)
+        bi_col = sb.tile([P, 2], F32, name="bi_col")
+        gm_col = sb.tile([P, 2], F32, name="gm_col")
+        ident = sb.tile([P, P], F32, name="ident")
+        one = sb.tile([P, 1], F32, name="one")
+        gap = [sb.tile([P, N + 1], F32, name="gap%d" % t) for t in range(TILES)]
+
+        def load_scales(engine, plane, scales, q):
+            passes = scales.shape[0]
+            engine.dma_start(
+                out=plane[32 * q : 32 * q + 4, :].bitcast(I32).rearrange("r (z c) -> r z c", z=passes),
+                in_=scales[:, 4 * q : 4 * q + 4, :].bitcast(I32).rearrange("z r c -> r z c"),
+            )
+
+        nc.vector.memset(xs[:].bitcast(I32), 0)
+        nc.vector.memset(one[:], 1.0)
+        nc.sync.dma_start(offsets[:], offs)
+        nc.sync.dma_start(out=xw[0][:].bitcast(I32), in_=xt_words[0].bitcast(I32))
+        nc.sync.dma_start(out=bi_col[:], in_=bi.rearrange("o (p c) -> (o p) c", c=2))
+        load_scales(nc.sync, xs, xt_scales, 0)
+        load_scales(nc.sync, xs, xt_scales, 1)
+        load_scales(nc.scalar, xs, xt_scales, 2)
+        load_scales(nc.scalar, xs, xt_scales, 3)
+        nc.sync.dma_start(out=raw[:], in_=sx.rearrange("(p t) j -> p t j", t=4))
+        nc.sync.dma_start(out=xw[1][:].bitcast(I32), in_=xt_words[1].bitcast(I32))
+        nc.sync.dma_start(out=waw[:].bitcast(I32).rearrange("p (z c) -> p z c", z=PASSES), in_=wa_words.rearrange("z p c t -> p z (c t)").bitcast(I32))
+        load_scales(nc.sync, was, wa_scales, 0)
+        load_scales(nc.sync, was, wa_scales, 1)
+        load_scales(nc.sync, was, wa_scales, 2)
+        load_scales(nc.sync, was, wa_scales, 3)
+        nc.sync.dma_start(out=wbw[:].bitcast(I32), in_=wb_words[0].rearrange("p c t -> p (c t)").bitcast(I32))
+        load_scales(nc.sync, wbs, wb_scales, 0)
+        load_scales(nc.gpsimd, wbs, wb_scales, 1)
+        load_scales(nc.gpsimd, wbs, wb_scales, 2)
+        make_identity(nc, ident[:])
+        load_scales(nc.gpsimd, wbs, wb_scales, 3)
+        nc.gpsimd.dma_start(out=gm_col[:], in_=gm.rearrange("o (p c) -> (o p) c", c=2))
+
+        for t in range(TILES):
+            nc.scalar.activation(gap[t][:, N : N + 1], one[:], ACT.Copy, scale=math.sqrt(OFFSET * N))
+
+        for z in range(PASSES):
+            nc.vector.tensor_copy(gs[z][:], xs[:, z * T : (z + 1) * T].indirect(offsets[:]))
+            nc.vector.tensor_copy(gw[z][:], xw[z][:].indirect(offsets[:]))
+
+        nc.scalar.copy(
+            out=grouped[:].rearrange("p (c i) t -> p c t i", i=4),
+            in_=raw[:].rearrange("p t (c i) -> p c t i", i=4),
+        )
+        nc.vector.quantize_mx(out=sxw[:].bitcast(E5M2), scales=sxs[:], in_=grouped[:].rearrange("p j t -> p (j t)"))
+
+        def spread(col, name, tag):
+            bank = ps.tile([P, 2, P], F32, name=name + "_bank")
+            for c in range(2):
+                nc.tensor.transpose(bank[:, c, :], col[:, c : c + 1].to_broadcast([P, P]), ident[:])
+            rows = sb.tile([P, N], F32, name=name + "_rows", tag=tag)
+            nc.scalar.copy(out=rows[:].rearrange("j (p c) -> j p c", c=2), in_=bank[:].rearrange("j c p -> j p c"))
+            return rows
+
+        bi_rows = spread(bi_col, "bi", "raw")
+
+        a = [ps.tile([P, N], F32, name="a%d" % t) for t in range(TILES)]
+        b = [ps.tile([P, N], F32, name="b%d" % t) for t in range(TILES)]
+        for t in range(TILES):
+            cols = slice(t * P, (t + 1) * P)
+            for z in range(PASSES):
+                nc.tensor.matmul_mx(
+                    a[t][:],
+                    lhsT=gw[z][:, cols].bitcast(E2M1),
+                    lhsT_scale=gs[z][:, cols],
+                    rhs=waw[:, z * N : (z + 1) * N].bitcast(E5M2),
+                    rhs_scale=was[:, z * N : (z + 1) * N],
+                    start=(z == 0),
+                    stop=(z == PASSES - 1),
+                )
+            nc.tensor.matmul_mx(
+                b[t][:],
+                lhsT=sxw[:, cols].bitcast(E5M2),
+                lhsT_scale=sxs[:, cols],
+                rhs=wbw[:].bitcast(E4M3),
+                rhs_scale=wbs[:],
+                start=True,
+                stop=True,
+            )
+        gm_rows = spread(gm_col, "gm", "gm_rows")
+
+        less_bias = [sb.tile([P, N], F32, name="less_bias%d" % t) for t in range(TILES)]
+        for t in range(TILES):
+            nc.vector.tensor_tensor(less_bias[t][:], a[t][:], bi_rows[:], ALU.subtract)
+            nc.vector.tensor_tensor(gap[t][:, 0:N], less_bias[t][:], b[t][:], ALU.subtract)
+        for t in range(TILES):
+            squares = sb.tile([P, N + 1], F32, name="squares%d" % t)
+            denom = sb.tile([P, 1], F32, name="denom%d" % t)
+            inverse = sb.tile([P, 1], F32, name="inverse%d" % t)
+            result = sb.tile([P, N], F32, name="result%d" % t)
+            nc.scalar.activation(squares[:], gap[t][:], ACT.Square, scale=1.0 / math.sqrt(N), accum_out=denom[:])
+            nc.vector.reciprocal(inverse[:], denom[:])
+            nc.vector.scalar_tensor_tensor(result[:], a[t][:], inverse[:], gm_rows[:], ALU.mult, ALU.mult)
+            nc.sync.dma_start(out=out[t * P : (t + 1) * P, :], in_=result[:])

@@ -34,22 +34,15 @@ def tile_list_rows_owninput_bygapsize_kernel(
         ps = ctx.enter_context(tc.psum_pool(name="ps", bufs=1))
 
         offsets = sb.tile([P, J // 16], U16, name="offsets")
-        xw = [sb.tile([P, T], U16, name="xw%d" % z, align_bytes=64) for z in range(PASSES)]
+        xw = [sb.tile([P, T], U16, name="xw0", align_bytes=64)]
         xs = sb.tile([P, PASSES * T], U8, name="xs", align_bytes=64)
         gw = [sb.tile([P, J], U16, name="gw%d" % z, align_bytes=64) for z in range(PASSES)]
         gs = [sb.tile([P, J], U8, name="gs%d" % z, align_bytes=64) for z in range(PASSES)]
-        waw = sb.tile([P, PASSES * N], U32, name="waw", align_bytes=64)
-        was = sb.tile([P, PASSES * N], U8, name="was", align_bytes=64)
-        wbw = sb.tile([P, N], U32, name="wbw", align_bytes=64)
-        wbs = sb.tile([P, N], U8, name="wbs", align_bytes=64)
-        raw = sb.tile([P, 4, J], F32, name="raw", tag="raw")
         grouped = sb.tile([P, J, 4], BF16, name="grouped", align_bytes=64)
         sxw = sb.tile([P, J], U32, name="sxw", align_bytes=64)
         sxs = sb.tile([P, J], U8, name="sxs", align_bytes=64)
         bi_col = sb.tile([P, 2], F32, name="bi_col")
-        gm_col = sb.tile([P, 2], F32, name="gm_col")
         ident = sb.tile([P, P], F32, name="ident")
-        one = sb.tile([P, 1], F32, name="one")
         gap = [sb.tile([P, N + 1], F32, name="gap%d" % t) for t in range(TILES)]
 
         def load_scales(engine, plane, scales, q):
@@ -60,7 +53,18 @@ def tile_list_rows_owninput_bygapsize_kernel(
             )
 
         nc.vector.memset(xs[:].bitcast(I32), 0)
-        nc.vector.memset(one[:], 1.0)
+        with tc.tile_pool(name="setup", bufs=1) as setup:
+            one = setup.tile([P, 1], F32, name="one")
+            nc.vector.memset(one[:], 1.0)
+            nc.vector.tensor_scalar(gap[0][:, N : N + 1], one[:], math.sqrt(OFFSET * N), None, ALU.mult)
+        late = ctx.enter_context(tc.tile_pool(name="late", bufs=1))
+        raw = late.tile([P, 4, J], F32, name="raw", tag="raw")
+        waw = late.tile([P, PASSES * N], U32, name="waw", align_bytes=64)
+        was = late.tile([P, PASSES * N], U8, name="was", align_bytes=64)
+        wbw = late.tile([P, N], U32, name="wbw", align_bytes=64)
+        wbs = late.tile([P, N], U8, name="wbs", align_bytes=64)
+        gm_col = late.tile([P, 2], F32, name="gm_col")
+        xw.append(late.tile([P, T], U16, name="xw1", align_bytes=64))
         nc.sync.dma_start(offsets[:], offs)
         nc.sync.dma_start(out=xw[0][:].bitcast(I32), in_=xt_words[0].bitcast(I32))
         nc.sync.dma_start(out=bi_col[:], in_=bi.rearrange("o (p c) -> (o p) c", c=2))
@@ -70,21 +74,20 @@ def tile_list_rows_owninput_bygapsize_kernel(
         load_scales(nc.scalar, xs, xt_scales, 3)
         nc.sync.dma_start(out=raw[:], in_=sx.rearrange("(p t) j -> p t j", t=4))
         nc.sync.dma_start(out=xw[1][:].bitcast(I32), in_=xt_words[1].bitcast(I32))
-        nc.sync.dma_start(out=waw[:].bitcast(I32).rearrange("p (z c) -> p z c", z=PASSES), in_=wa_words.rearrange("z p c t -> p z (c t)").bitcast(I32))
         load_scales(nc.sync, was, wa_scales, 0)
+        nc.sync.dma_start(out=waw[:].bitcast(I32).rearrange("p (z c) -> p z c", z=PASSES), in_=wa_words.rearrange("z p c t -> p z (c t)").bitcast(I32))
         load_scales(nc.sync, was, wa_scales, 1)
         load_scales(nc.sync, was, wa_scales, 2)
         load_scales(nc.sync, was, wa_scales, 3)
         nc.sync.dma_start(out=wbw[:].bitcast(I32), in_=wb_words[0].rearrange("p c t -> p (c t)").bitcast(I32))
         load_scales(nc.sync, wbs, wb_scales, 0)
+        load_scales(nc.sync, wbs, wb_scales, 3)
+        nc.sync.dma_start(out=gm_col[:], in_=gm.rearrange("o (p c) -> (o p) c", c=2))
+        make_identity(nc, ident[:])
         load_scales(nc.gpsimd, wbs, wb_scales, 1)
         load_scales(nc.gpsimd, wbs, wb_scales, 2)
-        make_identity(nc, ident[:])
-        load_scales(nc.gpsimd, wbs, wb_scales, 3)
-        nc.gpsimd.dma_start(out=gm_col[:], in_=gm.rearrange("o (p c) -> (o p) c", c=2))
 
-        for t in range(TILES):
-            nc.scalar.activation(gap[t][:, N : N + 1], one[:], ACT.Copy, scale=math.sqrt(OFFSET * N))
+        nc.scalar.activation(gap[1][:, N : N + 1], gap[0][:, N : N + 1], ACT.Copy)
 
         for z in range(PASSES):
             nc.vector.tensor_copy(gs[z][:], xs[:, z * T : (z + 1) * T].indirect(offsets[:]))
@@ -96,15 +99,18 @@ def tile_list_rows_owninput_bygapsize_kernel(
         )
         nc.vector.quantize_mx(out=sxw[:].bitcast(E5M2), scales=sxs[:], in_=grouped[:].rearrange("p j t -> p (j t)"))
 
-        def spread(col, name, tag):
-            bank = ps.tile([P, 2, P], F32, name=name + "_bank")
+        def spread(col, name):
+            bank = ps.tile([P, 2, P], F32, name=name)
             for c in range(2):
                 nc.tensor.transpose(bank[:, c, :], col[:, c : c + 1].to_broadcast([P, P]), ident[:])
-            rows = sb.tile([P, N], F32, name=name + "_rows", tag=tag)
-            nc.scalar.copy(out=rows[:].rearrange("j (p c) -> j p c", c=2), in_=bank[:].rearrange("j c p -> j p c"))
-            return rows
+            return bank[:].rearrange("j c p -> j p c")
 
-        bi_rows = spread(bi_col, "bi", "raw")
+        def pairs(tile):
+            return tile[:].rearrange("j (p c) -> j p c", c=2)
+
+        bi_bank = spread(bi_col, "bi_bank")
+        bi_rows = late.tile([P, N], F32, name="bi_rows", tag="raw")
+        nc.scalar.copy(out=pairs(bi_rows), in_=bi_bank)
 
         a = [ps.tile([P, N], F32, name="a%d" % t) for t in range(TILES)]
         b = [ps.tile([P, N], F32, name="b%d" % t) for t in range(TILES)]
@@ -120,6 +126,8 @@ def tile_list_rows_owninput_bygapsize_kernel(
                     start=(z == 0),
                     stop=(z == PASSES - 1),
                 )
+        for t in range(TILES):
+            cols = slice(t * P, (t + 1) * P)
             nc.tensor.matmul_mx(
                 b[t][:],
                 lhsT=sxw[:, cols].bitcast(E5M2),
@@ -129,18 +137,24 @@ def tile_list_rows_owninput_bygapsize_kernel(
                 start=True,
                 stop=True,
             )
-        gm_rows = spread(gm_col, "gm", "gm_rows")
+        gm_bank = spread(gm_col, "gm_bank")
 
+        a_sb = [sb.tile([P, N], F32, name="a_sb%d" % t) for t in range(TILES)]
         less_bias = [sb.tile([P, N], F32, name="less_bias%d" % t) for t in range(TILES)]
         for t in range(TILES):
             nc.vector.tensor_tensor(less_bias[t][:], a[t][:], bi_rows[:], ALU.subtract)
+            nc.scalar.copy(out=a_sb[t][:], in_=a[t][:])
+        for t in range(TILES):
             nc.vector.tensor_tensor(gap[t][:, 0:N], less_bias[t][:], b[t][:], ALU.subtract)
+        scaled = [sb.tile([P, N], F32, name="scaled%d" % t) for t in range(TILES)]
+        inverse = [sb.tile([P, 1], F32, name="inverse%d" % t) for t in range(TILES)]
         for t in range(TILES):
             squares = sb.tile([P, N + 1], F32, name="squares%d" % t)
             denom = sb.tile([P, 1], F32, name="denom%d" % t)
-            inverse = sb.tile([P, 1], F32, name="inverse%d" % t)
-            result = sb.tile([P, N], F32, name="result%d" % t)
             nc.scalar.activation(squares[:], gap[t][:], ACT.Square, scale=1.0 / math.sqrt(N), accum_out=denom[:])
-            nc.vector.reciprocal(inverse[:], denom[:])
-            nc.vector.scalar_tensor_tensor(result[:], a[t][:], inverse[:], gm_rows[:], ALU.mult, ALU.mult)
+            nc.vector.tensor_tensor(pairs(scaled[t]), pairs(a_sb[t]), gm_bank, ALU.mult)
+            nc.vector.reciprocal(inverse[t][:], denom[:])
+        for t in range(TILES):
+            result = sb.tile([P, N], F32, name="result%d" % t)
+            nc.vector.tensor_scalar(result[:], scaled[t][:], inverse[t][:], None, ALU.mult)
             nc.sync.dma_start(out=out[t * P : (t + 1) * P, :], in_=result[:])

import math
from contextlib import ExitStack

import concourse.mybir as mybir
from concourse.masks import make_identity

K, T, J, N, L = 1024, 1024, 256, 256, 512
FLOPS = 2 * J * K * N + 2 * J * L * N

F32 = mybir.dt.float32
BF16 = mybir.dt.bfloat16
I32 = mybir.dt.int32
U32 = mybir.dt.uint32
U16 = mybir.dt.uint16
U8 = mybir.dt.uint8
E2M1 = mybir.dt.float4_e2m1fn_x4
E5M2 = mybir.dt.float8_e5m2_x4
E4M3 = mybir.dt.float8_e4m3fn_x4
ALU = mybir.AluOpType
ACT = mybir.ActivationFunctionType

P = 128
PASSES = K // 512
TILES = J // P
OFFSET = 0.4


def tile_list_rows_owninput_bygapsize_kernel(
    tc, xt_words, xt_scales, wa_words, wa_scales, sx, wb_words, wb_scales, bi, gm, offs, out
):
    nc = tc.nc
    with ExitStack() as ctx:
        sb = ctx.enter_context(tc.tile_pool(name="sb", bufs=1))
        ps = ctx.enter_context(tc.psum_pool(name="ps", bufs=1))

        offsets = sb.tile([P, J // 16], U16, name="offsets")
        xw = [sb.tile([P, T], U16, name="xw0", align_bytes=64)]
        xs = sb.tile([P, PASSES * T], U8, name="xs", align_bytes=64)
        gw = [sb.tile([P, J], U16, name="gw%d" % z, align_bytes=64) for z in range(PASSES)]
        gs = [sb.tile([P, J], U8, name="gs%d" % z, align_bytes=64) for z in range(PASSES)]
        grouped = sb.tile([P, J, 4], BF16, name="grouped", align_bytes=64)
        sxw = sb.tile([P, J], U32, name="sxw", align_bytes=64)
        sxs = sb.tile([P, J], U8, name="sxs", align_bytes=64)
        bi_col = sb.tile([P, 2], F32, name="bi_col")
        ident = sb.tile([P, P], F32, name="ident")
        gap = [sb.tile([P, N + 1], F32, name="gap%d" % t) for t in range(TILES)]

        def load_scales(engine, plane, scales, q):
            passes = scales.shape[0]
            engine.dma_start(
                out=plane[32 * q : 32 * q + 4, :].bitcast(I32).rearrange("r (z c) -> r z c", z=passes),
                in_=scales[:, 4 * q : 4 * q + 4, :].bitcast(I32).rearrange("z r c -> r z c"),
            )

        nc.vector.memset(xs[:].bitcast(I32), 0)
        with tc.tile_pool(name="setup", bufs=1) as setup:
            one = setup.tile([P, 1], F32, name="one")
            nc.vector.memset(one[:], 1.0)
            nc.vector.tensor_scalar(gap[0][:, N : N + 1], one[:], math.sqrt(OFFSET * N), None, ALU.mult)
        late = ctx.enter_context(tc.tile_pool(name="late", bufs=1))
        raw = late.tile([P, 4, J], F32, name="raw", tag="raw")
        waw = late.tile([P, PASSES * N], U32, name="waw", align_bytes=64)
        was = late.tile([P, PASSES * N], U8, name="was", align_bytes=64)
        wbw = late.tile([P, N], U32, name="wbw", align_bytes=64)
        wbs = late.tile([P, N], U8, name="wbs", align_bytes=64)
        gm_col = late.tile([P, 2], F32, name="gm_col")
        xw.append(late.tile([P, T], U16, name="xw1", align_bytes=64))
        nc.sync.dma_start(offsets[:], offs)
        nc.sync.dma_start(out=xw[0][:].bitcast(I32), in_=xt_words[0].bitcast(I32))
        nc.sync.dma_start(out=bi_col[:], in_=bi.rearrange("o (p c) -> (o p) c", c=2))
        load_scales(nc.sync, xs, xt_scales, 0)
        load_scales(nc.sync, xs, xt_scales, 1)
        load_scales(nc.scalar, xs, xt_scales, 2)
        load_scales(nc.scalar, xs, xt_scales, 3)
        nc.sync.dma_start(out=raw[:], in_=sx.rearrange("(p t) j -> p t j", t=4))
        nc.sync.dma_start(out=xw[1][:].bitcast(I32), in_=xt_words[1].bitcast(I32))
        load_scales(nc.sync, was, wa_scales, 0)
        nc.sync.dma_start(out=waw[:].bitcast(I32).rearrange("p (z c) -> p z c", z=PASSES), in_=wa_words.rearrange("z p c t -> p z (c t)").bitcast(I32))
        load_scales(nc.sync, was, wa_scales, 1)
        load_scales(nc.sync, was, wa_scales, 2)
        load_scales(nc.sync, was, wa_scales, 3)
        nc.sync.dma_start(out=wbw[:].bitcast(I32), in_=wb_words[0].rearrange("p c t -> p (c t)").bitcast(I32))
        load_scales(nc.sync, wbs, wb_scales, 0)
        load_scales(nc.sync, wbs, wb_scales, 3)
        nc.sync.dma_start(out=gm_col[:], in_=gm.rearrange("o (p c) -> (o p) c", c=2))
        make_identity(nc, ident[:])
        load_scales(nc.gpsimd, wbs, wb_scales, 1)
        load_scales(nc.gpsimd, wbs, wb_scales, 2)

        nc.scalar.activation(gap[1][:, N : N + 1], gap[0][:, N : N + 1], ACT.Copy)

        for z in range(PASSES):
            nc.vector.tensor_copy(gs[z][:], xs[:, z * T : (z + 1) * T].indirect(offsets[:]))
            nc.vector.tensor_copy(gw[z][:], xw[z][:].indirect(offsets[:]))

        nc.scalar.copy(
            out=grouped[:].rearrange("p (c i) t -> p c t i", i=4),
            in_=raw[:].rearrange("p t (c i) -> p c t i", i=4),
        )
        nc.vector.quantize_mx(out=sxw[:].bitcast(E5M2), scales=sxs[:], in_=grouped[:].rearrange("p j t -> p (j t)"))

        def spread(col, name):
            bank = ps.tile([P, 2, P], F32, name=name)
            for c in range(2):
                nc.tensor.transpose(bank[:, c, :], col[:, c : c + 1].to_broadcast([P, P]), ident[:])
            return bank[:].rearrange("j c p -> j p c")

        def pairs(tile):
            return tile[:].rearrange("j (p c) -> j p c", c=2)

        bi_bank = spread(bi_col, "bi_bank")
        bi_rows = late.tile([P, N], F32, name="bi_rows", tag="raw")
        nc.scalar.copy(out=pairs(bi_rows), in_=bi_bank)

        a = [ps.tile([P, N], F32, name="a%d" % t) for t in range(TILES)]
        b = [ps.tile([P, N], F32, name="b%d" % t) for t in range(TILES)]
        for t in range(TILES):
            cols = slice(t * P, (t + 1) * P)
            for z in range(PASSES):
                nc.tensor.matmul_mx(
                    a[t][:],
                    lhsT=gw[z][:, cols].bitcast(E2M1),
                    lhsT_scale=gs[z][:, cols],
                    rhs=waw[:, z * N : (z + 1) * N].bitcast(E5M2),
                    rhs_scale=was[:, z * N : (z + 1) * N],
                    start=(z == 0),
                    stop=(z == PASSES - 1),
                )
        for t in range(TILES):
            cols = slice(t * P, (t + 1) * P)
            nc.tensor.matmul_mx(
                b[t][:],
                lhsT=sxw[:, cols].bitcast(E5M2),
                lhsT_scale=sxs[:, cols],
                rhs=wbw[:].bitcast(E4M3),
                rhs_scale=wbs[:],
                start=True,
                stop=True,
            )
        gm_bank = spread(gm_col, "gm_bank")

        a_sb = [sb.tile([P, N], F32, name="a_sb%d" % t) for t in range(TILES)]
        less_bias = [sb.tile([P, N], F32, name="less_bias%d" % t) for t in range(TILES)]
        for t in range(TILES):
            nc.vector.tensor_tensor(less_bias[t][:], a[t][:], bi_rows[:], ALU.subtract)
            nc.scalar.copy(out=a_sb[t][:], in_=a[t][:])
        for t in range(TILES):
            nc.vector.tensor_tensor(gap[t][:, 0:N], less_bias[t][:], b[t][:], ALU.subtract)
        scaled = [sb.tile([P, N], F32, name="scaled%d" % t) for t in range(TILES)]
        inverse = [sb.tile([P, 1], F32, name="inverse%d" % t) for t in range(TILES)]
        for t in range(TILES):
            squares = sb.tile([P, N + 1], F32, name="squares%d" % t)
            denom = sb.tile([P, 1], F32, name="denom%d" % t)
            nc.scalar.activation(squares[:], gap[t][:], ACT.Square, scale=1.0 / math.sqrt(N), accum_out=denom[:])
            nc.vector.tensor_tensor(pairs(scaled[t]), pairs(a_sb[t]), gm_bank, ALU.mult)
            nc.vector.reciprocal(inverse[t][:], denom[:])
        for t in range(TILES):
            result = sb.tile([P, N], F32, name="result%d" % t)
            nc.vector.tensor_scalar(result[:], scaled[t][:], inverse[t][:], None, ALU.mult)
            nc.sync.dma_start(out=out[t * P : (t + 1) * P, :], in_=result[:])
